import numpy as np
import ml_dtypes


def mxq(x, axis, fmt="e4m3"):
    dtype, down = {"e4m3": (ml_dtypes.float8_e4m3fn, 7), "e5m2": (ml_dtypes.float8_e5m2, 14)}[fmt]
    v = np.moveaxis(np.asarray(x, np.float32).astype(ml_dtypes.bfloat16).astype(np.float64), axis, -1)
    blocks = v.reshape(v.shape[:-1] + (-1, 32))
    amax = np.abs(blocks).max(-1, keepdims=True)
    byte = np.maximum(np.where(amax > 0, np.frexp(amax)[1] - 1 + 127, 0) - down, 1)
    scale = np.exp2(byte - 127.0)
    codes = (blocks / scale).astype(np.float32).astype(dtype).astype(np.float64)
    return np.moveaxis((codes * scale).reshape(v.shape), -1, axis)


WIDE = False


def mx_kscale(k):
    if not WIDE:
        return np.ones(k)
    levels = np.array([30, -30])
    if k % 512:
        return np.exp2(np.random.permutation(np.resize(levels, k // 32))).repeat(32)
    a = np.empty((k // 512, 16))
    for p in range(k // 512):
        a[p, :8] = np.random.permutation(np.resize(levels, 8))
        for g in range(8):
            far = levels[np.abs(levels - a[p, g]) >= 10]
            a[p, g + 8] = far[np.random.randint(len(far))]
    return np.exp2(a.ravel()).repeat(32)


def f64(x):
    return np.asarray(x).astype(np.float64)


def striped(idx):
    return np.tile(np.asarray(idx).reshape(-1, 16).T, (8, 1)).astype(np.uint16)


def unstriped(offs):
    return offs[:16].T.reshape(-1).astype(np.int64)


K, N, T, J = 512, 512, 2048, 512


def setup_inputs():
    n = np.random.standard_normal
    idx = np.random.permutation(T)[:J]
    fj = mx_kscale(J)
    tj = np.ones(T)
    tj[idx] = fj
    return {
        "xt": (n((K, T)) * tj).astype(np.float32),
        "g": (n((N, T)) * np.exp(0.7 * n((1, T))) / tj).astype(np.float32),
        "mom": (1.0 * n((K, N))).astype(np.float32),
        "old": (1.0 * n((K, N))).astype(np.float32),
        "offs": striped(idx),
    }


def reference(xt, g, mom, old, offs):
    idx = unstriped(offs)
    xj = f64(xt)[:, idx].T
    gj = f64(g)[:, idx].T
    xjq = mxq(xj, 0, "e4m3")
    gjq = mxq(gj, 0, "e5m2")
    w = xjq.T @ gjq
    u = 0.04 * w + 0.5 * f64(mom)
    y = 0.3 * f64(old) - u / (np.abs(u) + np.mean(np.abs(u), axis=1, keepdims=True))
    return y

@@ -1,0 +1,176 @@
+from contextlib import ExitStack
+
+import concourse.mybir as mybir
+from concourse.masks import make_identity
+
+K, N, T, J = 512, 512, 2048, 512
+FLOPS = 2 * K * N * J
+
+F32 = mybir.dt.float32
+BF16 = mybir.dt.bfloat16
+U32 = mybir.dt.uint32
+U16 = mybir.dt.uint16
+U8 = mybir.dt.uint8
+E4M3 = mybir.dt.float8_e4m3fn_x4
+E5M2 = mybir.dt.float8_e5m2_x4
+ALU = mybir.AluOpType
+ACT = mybir.ActivationFunctionType
+
+P = 128
+B = 4
+
+
+def tile_moe_expert_soft_sign_step_kernel(tc, xt, g, mom, old, offs, out):
+    nc = tc.nc
+    x_rows = xt.rearrange("(p b) t -> p b t", b=B)
+    mom_rows = mom.rearrange("(p b) n -> p b n", b=B)
+    old_rows = old.rearrange("(p b) n -> p b n", b=B)
+    out_rows = out.rearrange("(p b) n -> p b n", b=B)
+
+    with ExitStack() as ctx:
+        keep = ctx.enter_context(tc.tile_pool(name="keep", bufs=1))
+        turn = ctx.enter_context(tc.psum_pool(name="turn", bufs=3))
+        sums = ctx.enter_context(tc.psum_pool(name="sums", bufs=4))
+
+        offsets = keep.tile([P, J // 16], U16, name="offsets")
+        nc.sync.dma_start(offsets[:], offs)
+
+        warm = keep.tile([P, 1], F32, name="warm")
+        nc.vector.memset(warm[:], 1.0)
+        warm2 = keep.tile([P, 1], F32, name="warm2")
+        nc.scalar.activation(warm2[:], warm[:], ACT.Abs_reciprocal_sqrt)
+
+        ident = keep.tile([P, P], F32, name="ident")
+        make_identity(nc, ident[:])
+
+        g_win = [keep.tile([P, T], F32, name=f"g_win{c}", align_bytes=64) for c in range(B)]
+        x_win = [keep.tile([P, T], F32, name=f"x_win{b}", align_bytes=64) for b in range(B)]
+        mom01 = keep.tile([P, 2, N], F32, name="mom01", align_bytes=64)
+        mom2 = keep.tile([P, N], F32, name="mom2", align_bytes=64)
+        mom3 = keep.tile([P, N], F32, name="mom3", align_bytes=64)
+        mom_t = [mom01[:, 0, :], mom01[:, 1, :], mom2[:], mom3[:]]
+        old_t = [keep.tile([P, 2, N], F32, name=f"old{h}", align_bytes=64) for h in range(2)]
+        for c in range(B):
+            nc.sync.dma_start(g_win[c][:], g[c * P : (c + 1) * P, :])
+        nc.sync.dma_start(x_win[0][:], x_rows[:, 0, :])
+        nc.sync.dma_start(x_win[1][:], x_rows[:, 1, :])
+        nc.sync.dma_start(x_win[2][:], x_rows[:, 2, :])
+        nc.sync.dma_start(mom01[:], mom_rows[:, 0:2, :])
+        nc.sync.dma_start(x_win[3][:], x_rows[:, 3, :])
+        nc.sync.dma_start(mom2[:], mom_rows[:, 2, :])
+        nc.sync.dma_start(mom3[:], mom_rows[:, 3, :])
+        nc.sync.dma_start(old_t[0][:], old_rows[:, 0:2, :])
+        nc.sync.dma_start(old_t[1][:], old_rows[:, 2:4, :])
+
+        def gather_turn(window, tag, grouped):
+            listed = keep.tile([P, J], BF16, name=f"listed_{tag}", align_bytes=64)
+            nc.vector.tensor_copy(listed[:], window[:].indirect(offsets[:]))
+            words = listed[:].bitcast(F32)
+            turned = turn.tile([P, 2, P], F32, name="turned")
+            for u in range(2):
+                nc.tensor.transpose(turned[:, u, :], words[:, u::2], ident[:])
+            nc.scalar.copy(
+                grouped.bitcast(F32).rearrange("p (r u) -> p r u", u=2),
+                turned[:].rearrange("p u r -> p r u"),
+            )
+
+        g_grouped = keep.tile([P, 4 * N], BF16, name="g_grouped", align_bytes=64)
+        for c in range(B):
+            gather_turn(g_win[c], f"g{c}", g_grouped[:, c * 4 * P : (c + 1) * 4 * P])
+        x_grouped = [keep.tile([P, 4 * P], BF16, name=f"x_grouped{b}", align_bytes=64) for b in range(B)]
+        gather_turn(x_win[0], "x0", x_grouped[0][:])
+        g_codes = keep.tile([P, N], U32, name="g_codes", tag="x_win0", align_bytes=64)
+        g_scales = keep.tile([P, N], U8, name="g_scales", align_bytes=64)
+        nc.vector.quantize_mx(g_codes[:].bitcast(E5M2), g_scales[:], g_grouped[:])
+
+        acc = {}
+        mixed = {}
+        inv = {}
+        step = {}
+
+        def product(b, tag):
+            grouped = x_grouped[b]
+            codes = keep.tile([P, P], U32, name=f"x_codes{b}", tag=tag, align_bytes=64)
+            scales = keep.tile([P, P], U8, name=f"x_scales{b}", align_bytes=64)
+            nc.vector.quantize_mx(codes[:].bitcast(E4M3), scales[:], grouped[:])
+            acc[b] = sums.tile([P, N], F32, name="acc")
+            nc.tensor.matmul_mx(
+                acc[b][:], lhsT=codes[:].bitcast(E4M3), lhsT_scale=scales[:],
+                rhs=g_codes[:].bitcast(E5M2), rhs_scale=g_scales[:], start=True, stop=True,
+            )
+
+        def mix(b, tag):
+            mixed[b] = keep.tile([P, N], F32, name=f"mixed{b}", tag=tag, align_bytes=64)
+            nc.vector.scalar_tensor_tensor(
+                mixed[b][:], acc[b][:], 0.04 / 0.5, mom_t[b], ALU.mult, ALU.add
+            )
+
+        share = {}
+        mean = {}
+        root = {}
+
+        def magnitude(b):
+            share[b] = keep.tile([P, N], F32, name=f"share{b}")
+            mean[b] = keep.tile([P, 1], F32, name=f"mean{b}")
+            root[b] = keep.tile([P, N], F32, name=f"root{b}")
+            inv[b] = keep.tile([P, N], F32, name=f"inv{b}")
+            nc.scalar.activation(share[b][:], mixed[b][:], ACT.Abs, scale=1.0 / N, accum_out=mean[b][:])
+
+        def inverse_root(b, cols):
+            nc.scalar.activation(
+                root[b][:, cols], share[b][:, cols], ACT.Abs_reciprocal_sqrt, bias=mean[b][:], scale=float(N)
+            )
+
+        def square(b, cols):
+            nc.scalar.activation(inv[b][:, cols], root[b][:, cols], ACT.Square)
+
+        def ratio(b, cols, tag):
+            if b not in step:
+                step[b] = keep.tile([P, N], F32, name=f"step{b}", tag=tag, align_bytes=64)
+            nc.vector.tensor_tensor(step[b][:, cols], mixed[b][:, cols], inv[b][:, cols], ALU.mult)
+
+        def finish(b, cols, tag):
+            width = cols.stop - cols.start
+            y = keep.tile([P, width], F32, name=f"y{tag}")
+            nc.vector.scalar_tensor_tensor(
+                y[:], old_t[b // 2][:, b % 2, cols], 0.3, step[b][:, cols], ALU.mult, ALU.subtract
+            )
+            nc.sync.dma_start(out_rows[:, b, cols], y[:])
+
+        whole = slice(0, N)
+        halves = [slice(0, N // 2), slice(N // 2, N)]
+        gather_turn(x_win[1], "x1", x_grouped[1][:])
+        product(0, "x_win1")
+        gather_turn(x_win[2], "x2", x_grouped[2][:])
+        product(1, "x_win2")
+        mix(0, "mixed0")
+        mix(1, "mixed1")
+        product(2, "x_codes2")
+        magnitude(0)
+        magnitude(1)
+        inverse_root(0, whole)
+        inverse_root(1, whole)
+        square(0, whole)
+        gather_turn(x_win[3], "x3", x_grouped[3][:])
+        mix(2, "mixed2")
+        product(3, "x_codes3")
+        mix(3, "mixed3")
+        magnitude(2)
+        square(1, whole)
+        inverse_root(2, whole)
+        square(2, whole)
+        magnitude(3)
+        for h in range(2):
+            inverse_root(3, halves[h])
+        for h in range(2):
+            square(3, halves[h])
+        ratio(0, whole, "mom2")
+        finish(0, whole, "0")
+        ratio(1, whole, "step1")
+        ratio(2, whole, "step2")
+        finish(1, whole, "1")
+        finish(2, whole, "2")
+        for h in range(2):
+            ratio(3, halves[h], "step3")
+        for h in range(2):
+            finish(3, halves[h], f"3{h}")

@@ -29,11 +29,11 @@ def tile_moe_expert_soft_sign_step_kernel(tc, xt, g, mom, old, offs, out):
 
     with ExitStack() as ctx:
         keep = ctx.enter_context(tc.tile_pool(name="keep", bufs=1))
+        last = ctx.enter_context(tc.tile_pool(name="last", bufs=1))
         turn = ctx.enter_context(tc.psum_pool(name="turn", bufs=3))
         sums = ctx.enter_context(tc.psum_pool(name="sums", bufs=4))
 
         offsets = keep.tile([P, J // 16], U16, name="offsets")
-        nc.sync.dma_start(offsets[:], offs)
 
         warm = keep.tile([P, 1], F32, name="warm")
         nc.vector.memset(warm[:], 1.0)
@@ -46,39 +46,49 @@ def tile_moe_expert_soft_sign_step_kernel(tc, xt, g, mom, old, offs, out):
         g_win = [keep.tile([P, T], F32, name=f"g_win{c}", align_bytes=64) for c in range(B)]
         x_win = [keep.tile([P, T], F32, name=f"x_win{b}", align_bytes=64) for b in range(B)]
         mom01 = keep.tile([P, 2, N], F32, name="mom01", align_bytes=64)
-        mom2 = keep.tile([P, N], F32, name="mom2", align_bytes=64)
+        mom2 = last.tile([P, N], F32, name="mom2", offset=1024)
         mom3 = keep.tile([P, N], F32, name="mom3", align_bytes=64)
         mom_t = [mom01[:, 0, :], mom01[:, 1, :], mom2[:], mom3[:]]
         old_t = [keep.tile([P, 2, N], F32, name=f"old{h}", align_bytes=64) for h in range(2)]
         for c in range(B):
             nc.sync.dma_start(g_win[c][:], g[c * P : (c + 1) * P, :])
+            if c == 0:
+                nc.sync.dma_start(offsets[:], offs)
         nc.sync.dma_start(x_win[0][:], x_rows[:, 0, :])
         nc.sync.dma_start(x_win[1][:], x_rows[:, 1, :])
         nc.sync.dma_start(x_win[2][:], x_rows[:, 2, :])
         nc.sync.dma_start(mom01[:], mom_rows[:, 0:2, :])
         nc.sync.dma_start(x_win[3][:], x_rows[:, 3, :])
         nc.sync.dma_start(mom2[:], mom_rows[:, 2, :])
-        nc.sync.dma_start(mom3[:], mom_rows[:, 3, :])
         nc.sync.dma_start(old_t[0][:], old_rows[:, 0:2, :])
+        nc.sync.dma_start(mom3[:], mom_rows[:, 3, :])
         nc.sync.dma_start(old_t[1][:], old_rows[:, 2:4, :])
 
-        def gather_turn(window, tag, grouped):
+        def gather_turn(window, tag):
             listed = keep.tile([P, J], BF16, name=f"listed_{tag}", align_bytes=64)
             nc.vector.tensor_copy(listed[:], window[:].indirect(offsets[:]))
             words = listed[:].bitcast(F32)
             turned = turn.tile([P, 2, P], F32, name="turned")
             for u in range(2):
                 nc.tensor.transpose(turned[:, u, :], words[:, u::2], ident[:])
-            nc.scalar.copy(
+            return turned
+
+        def weave(turned, grouped, move=nc.scalar.copy):
+            move(
                 grouped.bitcast(F32).rearrange("p (r u) -> p r u", u=2),
                 turned[:].rearrange("p u r -> p r u"),
             )
 
         g_grouped = keep.tile([P, 4 * N], BF16, name="g_grouped", align_bytes=64)
         for c in range(B):
-            gather_turn(g_win[c], f"g{c}", g_grouped[:, c * 4 * P : (c + 1) * 4 * P])
-        x_grouped = [keep.tile([P, 4 * P], BF16, name=f"x_grouped{b}", align_bytes=64) for b in range(B)]
-        gather_turn(x_win[0], "x0", x_grouped[0][:])
+            weave(gather_turn(g_win[c], f"g{c}"), g_grouped[:, c * 4 * P : (c + 1) * 4 * P])
+        x_grouped = {}
+
+        def weave_x(b, turned, tag, move=nc.scalar.copy):
+            x_grouped[b] = keep.tile([P, 4 * P], BF16, name=f"x_grouped{b}", tag=tag, align_bytes=64)
+            weave(turned, x_grouped[b][:], move)
+
+        weave_x(0, gather_turn(x_win[0], "x0"), "x_grouped0")
         g_codes = keep.tile([P, N], U32, name="g_codes", tag="x_win0", align_bytes=64)
         g_scales = keep.tile([P, N], U8, name="g_scales", align_bytes=64)
         nc.vector.quantize_mx(g_codes[:].bitcast(E5M2), g_scales[:], g_grouped[:])
@@ -88,9 +98,8 @@ def tile_moe_expert_soft_sign_step_kernel(tc, xt, g, mom, old, offs, out):
         inv = {}
         step = {}
 
-        def product(b, tag):
+        def product(b, codes):
             grouped = x_grouped[b]
-            codes = keep.tile([P, P], U32, name=f"x_codes{b}", tag=tag, align_bytes=64)
             scales = keep.tile([P, P], U8, name=f"x_scales{b}", align_bytes=64)
             nc.vector.quantize_mx(codes[:].bitcast(E4M3), scales[:], grouped[:])
             acc[b] = sums.tile([P, N], F32, name="acc")
@@ -109,11 +118,9 @@ def tile_moe_expert_soft_sign_step_kernel(tc, xt, g, mom, old, offs, out):
         mean = {}
         root = {}
 
-        def magnitude(b):
-            share[b] = keep.tile([P, N], F32, name=f"share{b}")
+        def magnitude(b, tag):
+            share[b] = keep.tile([P, N], F32, name=f"share{b}", tag=tag, align_bytes=64)
             mean[b] = keep.tile([P, 1], F32, name=f"mean{b}")
-            root[b] = keep.tile([P, N], F32, name=f"root{b}")
-            inv[b] = keep.tile([P, N], F32, name=f"inv{b}")
             nc.scalar.activation(share[b][:], mixed[b][:], ACT.Abs, scale=1.0 / N, accum_out=mean[b][:])
 
         def inverse_root(b, cols):
@@ -124,14 +131,12 @@ def tile_moe_expert_soft_sign_step_kernel(tc, xt, g, mom, old, offs, out):
         def square(b, cols):
             nc.scalar.activation(inv[b][:, cols], root[b][:, cols], ACT.Square)
 
-        def ratio(b, cols, tag):
-            if b not in step:
-                step[b] = keep.tile([P, N], F32, name=f"step{b}", tag=tag, align_bytes=64)
+        def ratio(b, cols):
             nc.vector.tensor_tensor(step[b][:, cols], mixed[b][:, cols], inv[b][:, cols], ALU.mult)
 
         def finish(b, cols, tag):
             width = cols.stop - cols.start
-            y = keep.tile([P, width], F32, name=f"y{tag}")
+            y = keep.tile([P, width], F32, name=f"y{b}", tag=tag, align_bytes=64)
             nc.vector.scalar_tensor_tensor(
                 y[:], old_t[b // 2][:, b % 2, cols], 0.3, step[b][:, cols], ALU.mult, ALU.subtract
             )
@@ -139,38 +144,50 @@ def tile_moe_expert_soft_sign_step_kernel(tc, xt, g, mom, old, offs, out):
 
         whole = slice(0, N)
         halves = [slice(0, N // 2), slice(N // 2, N)]
-        gather_turn(x_win[1], "x1", x_grouped[1][:])
-        product(0, "x_win1")
-        gather_turn(x_win[2], "x2", x_grouped[2][:])
-        product(1, "x_win2")
+        turned = gather_turn(x_win[1], "x1")
+        product(0, keep.tile([P, P], U32, name="x_codes0", tag="x_win1", align_bytes=64))
+        weave_x(1, turned, "x_grouped1")
+        turned = gather_turn(x_win[2], "x2")
+        product(1, keep.tile([P, P], U32, name="x_codes1", tag="x_win2", align_bytes=64))
+        weave_x(2, turned, "x_grouped2")
         mix(0, "mixed0")
+        product(2, keep.tile([P, P], U32, name="x_codes2", align_bytes=64))
         mix(1, "mixed1")
-        product(2, "x_codes2")
-        magnitude(0)
-        magnitude(1)
+        for b in range(B):
+            inv[b] = keep.tile([P, N], F32, name=f"inv{b}")
+        for b in (0, 2, 3):
+            root[b] = keep.tile([P, N], F32, name=f"root{b}")
+        magnitude(0, "share0")
         inverse_root(0, whole)
-        inverse_root(1, whole)
         square(0, whole)
-        gather_turn(x_win[3], "x3", x_grouped[3][:])
+        turned = gather_turn(x_win[3], "x3")
+        magnitude(1, "x_win3")
         mix(2, "mixed2")
-        product(3, "x_codes3")
-        mix(3, "mixed3")
-        magnitude(2)
-        square(1, whole)
+        step[0] = last.tile([P, N], F32, name="step0", offset=0)
+        ratio(0, whole)
+        weave_x(3, turned, "x_grouped3", nc.vector.tensor_copy)
+        product(3, keep.tile([P, P], U32, name="x_codes3", align_bytes=64))
+        magnitude(2, "share2")
+        root[1] = last.tile([P, N], F32, name="root1", offset=2048)
+        inverse_root(1, whole)
         inverse_root(2, whole)
+        square(1, whole)
         square(2, whole)
-        magnitude(3)
+        finish(0, whole, "x_grouped3")
+        mix(3, "mixed3")
+        magnitude(3, "share3")
         for h in range(2):
             inverse_root(3, halves[h])
         for h in range(2):
             square(3, halves[h])
-        ratio(0, whole, "mom2")
-        finish(0, whole, "0")
-        ratio(1, whole, "step1")
-        ratio(2, whole, "step2")
-        finish(1, whole, "1")
-        finish(2, whole, "2")
+        step[1] = keep.tile([P, N], F32, name="step1", tag="x_codes3", align_bytes=64)
+        step[2] = keep.tile([P, N], F32, name="step2")
+        step[3] = keep.tile([P, N], F32, name="step3")
+        ratio(1, whole)
+        ratio(2, whole)
+        finish(1, whole, "y1")
+        finish(2, whole, "y2")
         for h in range(2):
-            ratio(3, halves[h], "step3")
+            ratio(3, halves[h])
         for h in range(2):
-            finish(3, halves[h], f"3{h}")
+            finish(3, halves[h], f"y3{h}")

@@ -51,7 +51,8 @@ def tile_moe_expert_soft_sign_step_kernel(tc, xt, g, mom, old, offs, out):
         mom_t = [mom01[:, 0, :], mom01[:, 1, :], mom2[:], mom3[:]]
         old_t = [keep.tile([P, 2, N], F32, name=f"old{h}", align_bytes=64) for h in range(2)]
         for c in range(B):
-            nc.sync.dma_start(g_win[c][:], g[c * P : (c + 1) * P, :])
+            queue = nc.scalar if c % 2 else nc.sync
+            queue.dma_start(g_win[c][:], g[c * P : (c + 1) * P, :])
             if c == 0:
                 nc.sync.dma_start(offsets[:], offs)
         nc.sync.dma_start(x_win[0][:], x_rows[:, 0, :])

from contextlib import ExitStack

import concourse.mybir as mybir
from concourse.masks import make_identity

K, N, T, J = 512, 512, 2048, 512
FLOPS = 2 * K * N * J

F32 = mybir.dt.float32
BF16 = mybir.dt.bfloat16
U32 = mybir.dt.uint32
U16 = mybir.dt.uint16
U8 = mybir.dt.uint8
E4M3 = mybir.dt.float8_e4m3fn_x4
E5M2 = mybir.dt.float8_e5m2_x4
ALU = mybir.AluOpType
ACT = mybir.ActivationFunctionType

P = 128
B = 4


def tile_moe_expert_soft_sign_step_kernel(tc, xt, g, mom, old, offs, out):
    nc = tc.nc
    x_rows = xt.rearrange("(p b) t -> p b t", b=B)
    mom_rows = mom.rearrange("(p b) n -> p b n", b=B)
    old_rows = old.rearrange("(p b) n -> p b n", b=B)
    out_rows = out.rearrange("(p b) n -> p b n", b=B)

    with ExitStack() as ctx:
        keep = ctx.enter_context(tc.tile_pool(name="keep", bufs=1))
        last = ctx.enter_context(tc.tile_pool(name="last", bufs=1))
        turn = ctx.enter_context(tc.psum_pool(name="turn", bufs=3))
        sums = ctx.enter_context(tc.psum_pool(name="sums", bufs=4))

        offsets = keep.tile([P, J // 16], U16, name="offsets")

        warm = keep.tile([P, 1], F32, name="warm")
        nc.vector.memset(warm[:], 1.0)
        warm2 = keep.tile([P, 1], F32, name="warm2")
        nc.scalar.activation(warm2[:], warm[:], ACT.Abs_reciprocal_sqrt)

        ident = keep.tile([P, P], F32, name="ident")
        make_identity(nc, ident[:])

        g_win = [keep.tile([P, T], F32, name=f"g_win{c}", align_bytes=64) for c in range(B)]
        x_win = [keep.tile([P, T], F32, name=f"x_win{b}", align_bytes=64) for b in range(B)]
        mom01 = keep.tile([P, 2, N], F32, name="mom01", align_bytes=64)
        mom2 = last.tile([P, N], F32, name="mom2", offset=1024)
        mom3 = keep.tile([P, N], F32, name="mom3", align_bytes=64)
        mom_t = [mom01[:, 0, :], mom01[:, 1, :], mom2[:], mom3[:]]
        old_t = [keep.tile([P, 2, N], F32, name=f"old{h}", align_bytes=64) for h in range(2)]
        for c in range(B):
            queue = nc.scalar if c % 2 else nc.sync
            queue.dma_start(g_win[c][:], g[c * P : (c + 1) * P, :])
            if c == 0:
                nc.sync.dma_start(offsets[:], offs)
        nc.sync.dma_start(x_win[0][:], x_rows[:, 0, :])
        nc.sync.dma_start(x_win[1][:], x_rows[:, 1, :])
        nc.sync.dma_start(x_win[2][:], x_rows[:, 2, :])
        nc.sync.dma_start(mom01[:], mom_rows[:, 0:2, :])
        nc.sync.dma_start(x_win[3][:], x_rows[:, 3, :])
        nc.sync.dma_start(mom2[:], mom_rows[:, 2, :])
        nc.sync.dma_start(old_t[0][:], old_rows[:, 0:2, :])
        nc.sync.dma_start(mom3[:], mom_rows[:, 3, :])
        nc.sync.dma_start(old_t[1][:], old_rows[:, 2:4, :])

        def gather_turn(window, tag):
            listed = keep.tile([P, J], BF16, name=f"listed_{tag}", align_bytes=64)
            nc.vector.tensor_copy(listed[:], window[:].indirect(offsets[:]))
            words = listed[:].bitcast(F32)
            turned = turn.tile([P, 2, P], F32, name="turned")
            for u in range(2):
                nc.tensor.transpose(turned[:, u, :], words[:, u::2], ident[:])
            return turned

        def weave(turned, grouped, move=nc.scalar.copy):
            move(
                grouped.bitcast(F32).rearrange("p (r u) -> p r u", u=2),
                turned[:].rearrange("p u r -> p r u"),
            )

        g_grouped = keep.tile([P, 4 * N], BF16, name="g_grouped", align_bytes=64)
        for c in range(B):
            weave(gather_turn(g_win[c], f"g{c}"), g_grouped[:, c * 4 * P : (c + 1) * 4 * P])
        x_grouped = {}

        def weave_x(b, turned, tag, move=nc.scalar.copy):
            x_grouped[b] = keep.tile([P, 4 * P], BF16, name=f"x_grouped{b}", tag=tag, align_bytes=64)
            weave(turned, x_grouped[b][:], move)

        weave_x(0, gather_turn(x_win[0], "x0"), "x_grouped0")
        g_codes = keep.tile([P, N], U32, name="g_codes", tag="x_win0", align_bytes=64)
        g_scales = keep.tile([P, N], U8, name="g_scales", align_bytes=64)
        nc.vector.quantize_mx(g_codes[:].bitcast(E5M2), g_scales[:], g_grouped[:])

        acc = {}
        mixed = {}
        inv = {}
        step = {}

        def product(b, codes):
            grouped = x_grouped[b]
            scales = keep.tile([P, P], U8, name=f"x_scales{b}", align_bytes=64)
            nc.vector.quantize_mx(codes[:].bitcast(E4M3), scales[:], grouped[:])
            acc[b] = sums.tile([P, N], F32, name="acc")
            nc.tensor.matmul_mx(
                acc[b][:], lhsT=codes[:].bitcast(E4M3), lhsT_scale=scales[:],
                rhs=g_codes[:].bitcast(E5M2), rhs_scale=g_scales[:], start=True, stop=True,
            )

        def mix(b, tag):
            mixed[b] = keep.tile([P, N], F32, name=f"mixed{b}", tag=tag, align_bytes=64)
            nc.vector.scalar_tensor_tensor(
                mixed[b][:], acc[b][:], 0.04 / 0.5, mom_t[b], ALU.mult, ALU.add
            )

        share = {}
        mean = {}
        root = {}

        def magnitude(b, tag):
            share[b] = keep.tile([P, N], F32, name=f"share{b}", tag=tag, align_bytes=64)
            mean[b] = keep.tile([P, 1], F32, name=f"mean{b}")
            nc.scalar.activation(share[b][:], mixed[b][:], ACT.Abs, scale=1.0 / N, accum_out=mean[b][:])

        def inverse_root(b, cols):
            nc.scalar.activation(
                root[b][:, cols], share[b][:, cols], ACT.Abs_reciprocal_sqrt, bias=mean[b][:], scale=float(N)
            )

        def square(b, cols):
            nc.scalar.activation(inv[b][:, cols], root[b][:, cols], ACT.Square)

        def ratio(b, cols):
            nc.vector.tensor_tensor(step[b][:, cols], mixed[b][:, cols], inv[b][:, cols], ALU.mult)

        def finish(b, cols, tag):
            width = cols.stop - cols.start
            y = keep.tile([P, width], F32, name=f"y{b}", tag=tag, align_bytes=64)
            nc.vector.scalar_tensor_tensor(
                y[:], old_t[b // 2][:, b % 2, cols], 0.3, step[b][:, cols], ALU.mult, ALU.subtract
            )
            nc.sync.dma_start(out_rows[:, b, cols], y[:])

        whole = slice(0, N)
        halves = [slice(0, N // 2), slice(N // 2, N)]
        turned = gather_turn(x_win[1], "x1")
        product(0, keep.tile([P, P], U32, name="x_codes0", tag="x_win1", align_bytes=64))
        weave_x(1, turned, "x_grouped1")
        turned = gather_turn(x_win[2], "x2")
        product(1, keep.tile([P, P], U32, name="x_codes1", tag="x_win2", align_bytes=64))
        weave_x(2, turned, "x_grouped2")
        mix(0, "mixed0")
        product(2, keep.tile([P, P], U32, name="x_codes2", align_bytes=64))
        mix(1, "mixed1")
        for b in range(B):
            inv[b] = keep.tile([P, N], F32, name=f"inv{b}")
        for b in (0, 2, 3):
            root[b] = keep.tile([P, N], F32, name=f"root{b}")
        magnitude(0, "share0")
        inverse_root(0, whole)
        square(0, whole)
        turned = gather_turn(x_win[3], "x3")
        magnitude(1, "x_win3")
        mix(2, "mixed2")
        step[0] = last.tile([P, N], F32, name="step0", offset=0)
        ratio(0, whole)
        weave_x(3, turned, "x_grouped3", nc.vector.tensor_copy)
        product(3, keep.tile([P, P], U32, name="x_codes3", align_bytes=64))
        magnitude(2, "share2")
        root[1] = last.tile([P, N], F32, name="root1", offset=2048)
        inverse_root(1, whole)
        inverse_root(2, whole)
        square(1, whole)
        square(2, whole)
        finish(0, whole, "x_grouped3")
        mix(3, "mixed3")
        magnitude(3, "share3")
        for h in range(2):
            inverse_root(3, halves[h])
        for h in range(2):
            square(3, halves[h])
        step[1] = keep.tile([P, N], F32, name="step1", tag="x_codes3", align_bytes=64)
        step[2] = keep.tile([P, N], F32, name="step2")
        step[3] = keep.tile([P, N], F32, name="step3")
        ratio(1, whole)
        ratio(2, whole)
        finish(1, whole, "y1")
        finish(2, whole, "y2")
        for h in range(2):
            ratio(3, halves[h])
        for h in range(2):
            finish(3, halves[h], f"y3{h}")
